import numpy as np
import ml_dtypes

BF16 = ml_dtypes.bfloat16


def bf(x):
    return np.asarray(x, np.float32).astype(BF16)


def f32(x):
    return np.asarray(x, np.float32)


def f64(x):
    return np.asarray(x).astype(np.float64)


def striped(idx):
    return np.tile(idx.reshape(-1, 16).T, (8, 1))


S, K, M, N, D, V = 2048, 256, 128, 1536, 8, 192


def sigmoid(v):
    return 1.0 / (1.0 + np.exp(-v))


def setup_inputs():
    return {"table": bf(np.random.standard_normal((S, K))), "w": bf(np.random.standard_normal((K, M)) / np.sqrt(K)), "b": f32(0.5 * np.random.standard_normal((M, 1))), "offs": striped(np.random.permutation(np.tile(np.arange(S), 2))[:N])}


def reference(table, w, b, offs):
    idx = offs[:16].T.reshape(-1)
    x = f64(table)[idx].T
    y = f64(w).T @ x
    z = (y + f64(b)) * sigmoid(y + f64(b))
    return z.reshape(M, V, D).max(axis=2)

@@ -1,0 +1,75 @@
+import concourse.mybir as mybir
+from concourse.masks import make_identity
+
+BF16, F32, U16 = mybir.dt.bfloat16, mybir.dt.float32, mybir.dt.uint16
+
+P = 128
+S, K, M, N = 2048, 256, 128, 1536
+K_BLOCKS = K // P
+GROUP = 8
+PIECE = 512
+PIECES = N // PIECE
+ROWS = 512
+LOADS = S // ROWS
+FLOPS = 2 * K * M * N
+
+
+def tile_gather_matmul_kernel(tc, table, w, b, offs, out):
+    nc = tc.nc
+    with (
+        tc.tile_pool(name="held", bufs=1) as held,
+        tc.psum_pool(name="flip", bufs=4) as flip,
+        tc.psum_pool(name="sums", bufs=1) as sums,
+    ):
+        offsets = held.tile([P, N // 16], U16, name="offsets")
+        nc.sync.dma_start(offsets[:], offs)
+
+        weights = held.tile([P, K_BLOCKS, M], BF16, name="weights")
+        nc.scalar.dma_start(weights[:], w.rearrange("(a p) m -> p a m", p=P))
+        bias = held.tile([P, 1], F32, name="bias")
+        nc.scalar.dma_start(bias[:], b)
+
+        identity = held.tile([P, P], BF16, name="identity")
+        make_identity(nc, identity[:])
+
+        nodes = [held.tile([P, ROWS // P, K], BF16, name=f"nodes{g}") for g in range(LOADS)]
+        for g in range(LOADS):
+            nc.sync.dma_start(
+                nodes[g][:], table[g * ROWS : (g + 1) * ROWS, :].rearrange("(r p) k -> p r k", p=P)
+            )
+
+        windows = [held.tile([P, S], BF16, name=f"window{a}") for a in range(K_BLOCKS)]
+        for g in range(LOADS):
+            for a in range(K_BLOCKS):
+                flipped = flip.tile([P, ROWS], BF16, name="flipped")
+                for r in range(ROWS // P):
+                    nc.tensor.transpose(
+                        flipped[:, r * P : (r + 1) * P], nodes[g][:, r, a * P : (a + 1) * P], identity[:]
+                    )
+                target = windows[a][:, g * ROWS : (g + 1) * ROWS]
+                if a == 0:
+                    nc.vector.tensor_copy(target, flipped[:])
+                else:
+                    nc.scalar.copy(target, flipped[:])
+
+        banks = [sums.tile([P, PIECE], F32, name=f"bank{q}") for q in range(PIECES)]
+        for a in range(K_BLOCKS):
+            for q in range(PIECES):
+                picked = windows[a][:].indirect(offsets[:, q * (PIECE // 16) : (q + 1) * (PIECE // 16)])
+                nc.tensor.matmul(
+                    banks[q][:], weights[:, a, :], picked, start=(a == 0), stop=(a == K_BLOCKS - 1)
+                )
+
+        pooled = held.tile([P, N // GROUP], F32, name="pooled")
+        for q in range(PIECES):
+            activated = held.tile([P, PIECE], F32, name=f"activated{q}")
+            nc.scalar.activation(
+                activated[:], banks[q][:], mybir.ActivationFunctionType.Silu, bias=bias[:]
+            )
+            nc.vector.tensor_reduce(
+                pooled[:, q * (PIECE // GROUP) : (q + 1) * (PIECE // GROUP)],
+                activated[:].rearrange("p (v t) -> p v t", t=GROUP),
+                axis=mybir.AxisListType.X,
+                op=mybir.AluOpType.max,
+            )
+        nc.sync.dma_start(out, pooled[:])

@@ -2,15 +2,16 @@ import concourse.mybir as mybir
 from concourse.masks import make_identity
 
 BF16, F32, U16 = mybir.dt.bfloat16, mybir.dt.float32, mybir.dt.uint16
+SILU = mybir.ActivationFunctionType.Silu
 
 P = 128
 S, K, M, N = 2048, 256, 128, 1536
 K_BLOCKS = K // P
 GROUP = 8
-PIECE = 512
-PIECES = N // PIECE
-ROWS = 512
+PIECES = (512, 512, 256, 256)
+ROWS = 256
 LOADS = S // ROWS
+WARM_UPS = 4
 FLOPS = 2 * K * M * N
 
 
@@ -24,19 +25,30 @@ def tile_gather_matmul_kernel(tc, table, w, b, offs, out):
         offsets = held.tile([P, N // 16], U16, name="offsets")
         nc.sync.dma_start(offsets[:], offs)
 
-        weights = held.tile([P, K_BLOCKS, M], BF16, name="weights")
-        nc.scalar.dma_start(weights[:], w.rearrange("(a p) m -> p a m", p=P))
-        bias = held.tile([P, 1], F32, name="bias")
-        nc.scalar.dma_start(bias[:], b)
-
-        identity = held.tile([P, P], BF16, name="identity")
-        make_identity(nc, identity[:])
-
         nodes = [held.tile([P, ROWS // P, K], BF16, name=f"nodes{g}") for g in range(LOADS)]
         for g in range(LOADS):
             nc.sync.dma_start(
                 nodes[g][:], table[g * ROWS : (g + 1) * ROWS, :].rearrange("(r p) k -> p r k", p=P)
             )
+
+        weights = held.tile([P, K_BLOCKS, M], BF16, name="weights")
+        nc.scalar.dma_start(weights[:], w.rearrange("(a p) m -> p a m", p=P))
+        bias = held.tile([P, 1], F32, name="bias")
+        nc.scalar.dma_start(bias[:], b)
+
+        zeros = held.tile([P, 1], F32, name="zeros")
+        nc.vector.memset(zeros[:], 0.0)
+        unused = held.tile([P, 1], F32, name="unused")
+        nc.scalar.activation(unused[:], zeros[:], SILU)
+
+        identity = held.tile([P, P], BF16, name="identity")
+        make_identity(nc, identity[:])
+
+        idle = held.tile([P, PIECES[0]], BF16, name="idle")
+        nc.vector.memset(idle[:], 0.0)
+        warmed = flip.tile([P, PIECES[0]], F32, name="warmed", tag="flipped")
+        for i in range(WARM_UPS):
+            nc.tensor.matmul(warmed[:], idle[:, 0:P], idle[:], start=True, stop=True)
 
         windows = [held.tile([P, S], BF16, name=f"window{a}") for a in range(K_BLOCKS)]
         for g in range(LOADS):
@@ -52,24 +64,20 @@ def tile_gather_matmul_kernel(tc, table, w, b, offs, out):
                 else:
                     nc.scalar.copy(target, flipped[:])
 
-        banks = [sums.tile([P, PIECE], F32, name=f"bank{q}") for q in range(PIECES)]
-        for a in range(K_BLOCKS):
-            for q in range(PIECES):
-                picked = windows[a][:].indirect(offsets[:, q * (PIECE // 16) : (q + 1) * (PIECE // 16)])
-                nc.tensor.matmul(
-                    banks[q][:], weights[:, a, :], picked, start=(a == 0), stop=(a == K_BLOCKS - 1)
-                )
-
         pooled = held.tile([P, N // GROUP], F32, name="pooled")
-        for q in range(PIECES):
-            activated = held.tile([P, PIECE], F32, name=f"activated{q}")
-            nc.scalar.activation(
-                activated[:], banks[q][:], mybir.ActivationFunctionType.Silu, bias=bias[:]
-            )
+        first = 0
+        for q, width in enumerate(PIECES):
+            bank = sums.tile([P, width], F32, name=f"bank{q}")
+            for a in range(K_BLOCKS):
+                picked = windows[a][:].indirect(offsets[:, first // 16 : (first + width) // 16])
+                nc.tensor.matmul(bank[:], weights[:, a, :], picked, start=(a == 0), stop=(a == K_BLOCKS - 1))
+            activated = held.tile([P, width], F32, name=f"activated{q}")
+            nc.scalar.activation(activated[:], bank[:], SILU, bias=bias[:])
             nc.vector.tensor_reduce(
-                pooled[:, q * (PIECE // GROUP) : (q + 1) * (PIECE // GROUP)],
+                pooled[:, first // GROUP : (first + width) // GROUP],
                 activated[:].rearrange("p (v t) -> p v t", t=GROUP),
                 axis=mybir.AxisListType.X,
                 op=mybir.AluOpType.max,
             )
+            first += width
         nc.sync.dma_start(out, pooled[:])

@@ -44,14 +44,20 @@ def tile_gather_matmul_kernel(tc, table, w, b, offs, out):
         identity = held.tile([P, P], BF16, name="identity")
         make_identity(nc, identity[:])
 
+        banks = [sums.tile([P, width], F32, name=f"bank{q}") for q, width in enumerate(PIECES)]
+
         idle = held.tile([P, PIECES[0]], BF16, name="idle")
         nc.vector.memset(idle[:], 0.0)
-        warmed = flip.tile([P, PIECES[0]], F32, name="warmed", tag="flipped")
+
+        def multiply_zeros(q):
+            nc.tensor.matmul(banks[q][:], idle[:, 0:P], idle[:, 0 : PIECES[q]], start=True, stop=True)
+
         for i in range(WARM_UPS):
-            nc.tensor.matmul(warmed[:], idle[:, 0:P], idle[:], start=True, stop=True)
+            multiply_zeros(0)
 
         windows = [held.tile([P, S], BF16, name=f"window{a}") for a in range(K_BLOCKS)]
         for g in range(LOADS):
+            multiply_zeros(len(PIECES) - 1)
             for a in range(K_BLOCKS):
                 flipped = flip.tile([P, ROWS], BF16, name="flipped")
                 for r in range(ROWS // P):
@@ -67,12 +73,13 @@ def tile_gather_matmul_kernel(tc, table, w, b, offs, out):
         pooled = held.tile([P, N // GROUP], F32, name="pooled")
         first = 0
         for q, width in enumerate(PIECES):
-            bank = sums.tile([P, width], F32, name=f"bank{q}")
             for a in range(K_BLOCKS):
                 picked = windows[a][:].indirect(offsets[:, first // 16 : (first + width) // 16])
-                nc.tensor.matmul(bank[:], weights[:, a, :], picked, start=(a == 0), stop=(a == K_BLOCKS - 1))
+                nc.tensor.matmul(
+                    banks[q][:], weights[:, a, :], picked, start=(a == 0), stop=(a == K_BLOCKS - 1)
+                )
             activated = held.tile([P, width], F32, name=f"activated{q}")
-            nc.scalar.activation(activated[:], bank[:], SILU, bias=bias[:])
+            nc.scalar.activation(activated[:], banks[q][:], SILU, bias=bias[:])
             nc.vector.tensor_reduce(
                 pooled[:, first // GROUP : (first + width) // GROUP],
                 activated[:].rearrange("p (v t) -> p v t", t=GROUP),

@@ -11,6 +11,7 @@ GROUP = 8
 PIECES = (512, 512, 256, 256)
 ROWS = 256
 LOADS = S // ROWS
+PSUM_BANKS = 8
 WARM_UPS = 4
 FLOPS = 2 * K * M * N
 
@@ -19,22 +20,21 @@ def tile_gather_matmul_kernel(tc, table, w, b, offs, out):
     nc = tc.nc
     with (
         tc.tile_pool(name="held", bufs=1) as held,
-        tc.psum_pool(name="flip", bufs=4) as flip,
-        tc.psum_pool(name="sums", bufs=1) as sums,
+        tc.psum_pool(name="psum", bufs=PSUM_BANKS) as psum,
     ):
-        offsets = held.tile([P, N // 16], U16, name="offsets")
-        nc.sync.dma_start(offsets[:], offs)
-
         nodes = [held.tile([P, ROWS // P, K], BF16, name=f"nodes{g}") for g in range(LOADS)]
         for g in range(LOADS):
-            nc.sync.dma_start(
+            queue = nc.sync if g % 2 == 0 else nc.scalar
+            queue.dma_start(
                 nodes[g][:], table[g * ROWS : (g + 1) * ROWS, :].rearrange("(r p) k -> p r k", p=P)
             )
 
+        offsets = held.tile([P, N // 16], U16, name="offsets")
+        nc.sync.dma_start(offsets[:], offs)
         weights = held.tile([P, K_BLOCKS, M], BF16, name="weights")
-        nc.scalar.dma_start(weights[:], w.rearrange("(a p) m -> p a m", p=P))
+        nc.sync.dma_start(weights[:], w.rearrange("(a p) m -> p a m", p=P))
         bias = held.tile([P, 1], F32, name="bias")
-        nc.scalar.dma_start(bias[:], b)
+        nc.sync.dma_start(bias[:], b)
 
         zeros = held.tile([P, 1], F32, name="zeros")
         nc.vector.memset(zeros[:], 0.0)
@@ -44,22 +44,16 @@ def tile_gather_matmul_kernel(tc, table, w, b, offs, out):
         identity = held.tile([P, P], BF16, name="identity")
         make_identity(nc, identity[:])
 
-        banks = [sums.tile([P, width], F32, name=f"bank{q}") for q, width in enumerate(PIECES)]
-
         idle = held.tile([P, PIECES[0]], BF16, name="idle")
         nc.vector.memset(idle[:], 0.0)
-
-        def multiply_zeros(q):
-            nc.tensor.matmul(banks[q][:], idle[:, 0:P], idle[:, 0 : PIECES[q]], start=True, stop=True)
-
+        warmed = psum.tile([P, PIECES[0]], F32, name="warmed", tag="bank")
         for i in range(WARM_UPS):
-            multiply_zeros(0)
+            nc.tensor.matmul(warmed[:], idle[:, 0:P], idle[:], start=True, stop=True)
 
         windows = [held.tile([P, S], BF16, name=f"window{a}") for a in range(K_BLOCKS)]
         for g in range(LOADS):
-            multiply_zeros(len(PIECES) - 1)
             for a in range(K_BLOCKS):
-                flipped = flip.tile([P, ROWS], BF16, name="flipped")
+                flipped = psum.tile([P, ROWS], BF16, name="flipped", tag="bank")
                 for r in range(ROWS // P):
                     nc.tensor.transpose(
                         flipped[:, r * P : (r + 1) * P], nodes[g][:, r, a * P : (a + 1) * P], identity[:]
@@ -72,14 +66,13 @@ def tile_gather_matmul_kernel(tc, table, w, b, offs, out):
 
         pooled = held.tile([P, N // GROUP], F32, name="pooled")
         first = 0
-        for q, width in enumerate(PIECES):
+        for width in PIECES:
+            sums = psum.tile([P, width], F32, name="sums", tag="bank")
             for a in range(K_BLOCKS):
                 picked = windows[a][:].indirect(offsets[:, first // 16 : (first + width) // 16])
-                nc.tensor.matmul(
-                    banks[q][:], weights[:, a, :], picked, start=(a == 0), stop=(a == K_BLOCKS - 1)
-                )
-            activated = held.tile([P, width], F32, name=f"activated{q}")
-            nc.scalar.activation(activated[:], banks[q][:], SILU, bias=bias[:])
+                nc.tensor.matmul(sums[:], weights[:, a, :], picked, start=(a == 0), stop=(a == K_BLOCKS - 1))
+            activated = held.tile([P, width], F32, name=f"activated{first}")
+            nc.scalar.activation(activated[:], sums[:], SILU, bias=bias[:])
             nc.vector.tensor_reduce(
                 pooled[:, first // GROUP : (first + width) // GROUP],
                 activated[:].rearrange("p (v t) -> p v t", t=GROUP),

@@ -66,18 +66,21 @@ def tile_gather_matmul_kernel(tc, table, w, b, offs, out):
 
         pooled = held.tile([P, N // GROUP], F32, name="pooled")
         first = 0
-        for width in PIECES:
+        for piece, width in enumerate(PIECES):
             sums = psum.tile([P, width], F32, name="sums", tag="bank")
             for a in range(K_BLOCKS):
                 picked = windows[a][:].indirect(offsets[:, first // 16 : (first + width) // 16])
                 nc.tensor.matmul(sums[:], weights[:, a, :], picked, start=(a == 0), stop=(a == K_BLOCKS - 1))
-            activated = held.tile([P, width], F32, name=f"activated{first}")
-            nc.scalar.activation(activated[:], sums[:], SILU, bias=bias[:])
-            nc.vector.tensor_reduce(
-                pooled[:, first // GROUP : (first + width) // GROUP],
-                activated[:].rearrange("p (v t) -> p v t", t=GROUP),
-                axis=mybir.AxisListType.X,
-                op=mybir.AluOpType.max,
-            )
-            first += width
+            parts = 2 if piece == len(PIECES) - 1 else 1
+            part = width // parts
+            for h in range(parts):
+                activated = held.tile([P, part], F32, name=f"activated{first}")
+                nc.scalar.activation(activated[:], sums[:, h * part : (h + 1) * part], SILU, bias=bias[:])
+                nc.vector.tensor_reduce(
+                    pooled[:, first // GROUP : (first + part) // GROUP],
+                    activated[:].rearrange("p (v t) -> p v t", t=GROUP),
+                    axis=mybir.AxisListType.X,
+                    op=mybir.AluOpType.max,
+                )
+                first += part
         nc.sync.dma_start(out, pooled[:])

import concourse.mybir as mybir
from concourse.masks import make_identity

BF16, F32, U16 = mybir.dt.bfloat16, mybir.dt.float32, mybir.dt.uint16
SILU = mybir.ActivationFunctionType.Silu

P = 128
S, K, M, N = 2048, 256, 128, 1536
K_BLOCKS = K // P
GROUP = 8
PIECES = (512, 512, 256, 256)
ROWS = 256
LOADS = S // ROWS
PSUM_BANKS = 8
WARM_UPS = 4
FLOPS = 2 * K * M * N


def tile_gather_matmul_kernel(tc, table, w, b, offs, out):
    nc = tc.nc
    with (
        tc.tile_pool(name="held", bufs=1) as held,
        tc.psum_pool(name="psum", bufs=PSUM_BANKS) as psum,
    ):
        nodes = [held.tile([P, ROWS // P, K], BF16, name=f"nodes{g}") for g in range(LOADS)]
        for g in range(LOADS):
            queue = nc.sync if g % 2 == 0 else nc.scalar
            queue.dma_start(
                nodes[g][:], table[g * ROWS : (g + 1) * ROWS, :].rearrange("(r p) k -> p r k", p=P)
            )

        offsets = held.tile([P, N // 16], U16, name="offsets")
        nc.sync.dma_start(offsets[:], offs)
        weights = held.tile([P, K_BLOCKS, M], BF16, name="weights")
        nc.sync.dma_start(weights[:], w.rearrange("(a p) m -> p a m", p=P))
        bias = held.tile([P, 1], F32, name="bias")
        nc.sync.dma_start(bias[:], b)

        zeros = held.tile([P, 1], F32, name="zeros")
        nc.vector.memset(zeros[:], 0.0)
        unused = held.tile([P, 1], F32, name="unused")
        nc.scalar.activation(unused[:], zeros[:], SILU)

        identity = held.tile([P, P], BF16, name="identity")
        make_identity(nc, identity[:])

        idle = held.tile([P, PIECES[0]], BF16, name="idle")
        nc.vector.memset(idle[:], 0.0)
        warmed = psum.tile([P, PIECES[0]], F32, name="warmed", tag="bank")
        for i in range(WARM_UPS):
            nc.tensor.matmul(warmed[:], idle[:, 0:P], idle[:], start=True, stop=True)

        windows = [held.tile([P, S], BF16, name=f"window{a}") for a in range(K_BLOCKS)]
        for g in range(LOADS):
            for a in range(K_BLOCKS):
                flipped = psum.tile([P, ROWS], BF16, name="flipped", tag="bank")
                for r in range(ROWS // P):
                    nc.tensor.transpose(
                        flipped[:, r * P : (r + 1) * P], nodes[g][:, r, a * P : (a + 1) * P], identity[:]
                    )
                target = windows[a][:, g * ROWS : (g + 1) * ROWS]
                if a == 0:
                    nc.vector.tensor_copy(target, flipped[:])
                else:
                    nc.scalar.copy(target, flipped[:])

        pooled = held.tile([P, N // GROUP], F32, name="pooled")
        first = 0
        for piece, width in enumerate(PIECES):
            sums = psum.tile([P, width], F32, name="sums", tag="bank")
            for a in range(K_BLOCKS):
                picked = windows[a][:].indirect(offsets[:, first // 16 : (first + width) // 16])
                nc.tensor.matmul(sums[:], weights[:, a, :], picked, start=(a == 0), stop=(a == K_BLOCKS - 1))
            parts = 2 if piece == len(PIECES) - 1 else 1
            part = width // parts
            for h in range(parts):
                activated = held.tile([P, part], F32, name=f"activated{first}")
                nc.scalar.activation(activated[:], sums[:, h * part : (h + 1) * part], SILU, bias=bias[:])
                nc.vector.tensor_reduce(
                    pooled[:, first // GROUP : (first + part) // GROUP],
                    activated[:].rearrange("p (v t) -> p v t", t=GROUP),
                    axis=mybir.AxisListType.X,
                    op=mybir.AluOpType.max,
                )
                first += part
        nc.sync.dma_start(out, pooled[:])
